import numpy as np
import ml_dtypes


def mxq(x, axis, fmt="e4m3"):
    dtype, down = {"e4m3": (ml_dtypes.float8_e4m3fn, 7), "e5m2": (ml_dtypes.float8_e5m2, 14)}[fmt]
    v = np.moveaxis(np.asarray(x, np.float32).astype(ml_dtypes.bfloat16).astype(np.float64), axis, -1)
    blocks = v.reshape(v.shape[:-1] + (-1, 32))
    amax = np.abs(blocks).max(-1, keepdims=True)
    byte = np.maximum(np.where(amax > 0, np.frexp(amax)[1] - 1 + 127, 0) - down, 1)
    scale = np.exp2(byte - 127.0)
    codes = (blocks / scale).astype(np.float32).astype(dtype).astype(np.float64)
    return np.moveaxis((codes * scale).reshape(v.shape), -1, axis)


WIDE = False


def mx_kscale(k):
    if not WIDE:
        return np.ones(k)
    levels = np.array([10, -10, 5, -5, 0])
    if k % 512:
        return np.exp2(np.random.permutation(np.resize(levels, k // 32))).repeat(32)
    a = np.empty((k // 512, 16))
    for p in range(k // 512):
        a[p, :8] = np.random.permutation(np.resize(levels, 8))
        for g in range(8):
            far = levels[np.abs(levels - a[p, g]) >= 10]
            a[p, g + 8] = far[np.random.randint(len(far))]
    return np.exp2(a.ravel()).repeat(32)


BF16 = ml_dtypes.bfloat16


def bf(x):
    return np.asarray(x, np.float32).astype(BF16)


def f64(x):
    return np.asarray(x).astype(np.float64)


E2M1 = np.array([0.0, 0.5, 1.0, 1.5, 2.0, 3.0, 4.0, 6.0, -0.0, -0.5, -1.0, -1.5, -2.0, -3.0, -4.0, -6.0])


def pack_weight(w, fmt):
    k, n = w.shape
    w = f64(bf(w)).reshape(k // 32, 32, n)
    amax = np.abs(w).max(1)
    if fmt == "e4m3":
        byte = np.frexp(amax)[1] - 1 + 127 - 7
    else:
        mant, ex = np.frexp(amax / 6.0)
        byte = np.where(mant > 0.5, ex, ex - 1) + 127
    byte = np.clip(np.where(amax > 0, byte, 1), 1, 254)
    scaled = (w * np.exp2(127.0 - byte)[:, None, :]).reshape(k, n).astype(np.float32)
    by_word = np.ascontiguousarray(scaled.reshape(k // 512, 128, 4, n).transpose(0, 1, 3, 2))
    if fmt == "e4m3":
        words = by_word.astype(ml_dtypes.float8_e4m3fn).view(np.uint8)
    else:
        c = by_word.astype(ml_dtypes.float4_e2m1fn).view(np.uint8) & 0xF
        words = c[..., 0::2] | (c[..., 1::2] << 4)
    return np.ascontiguousarray(words), np.ascontiguousarray(byte.astype(np.uint8).reshape(k // 512, 16, n))


def unpack_weight(words, scales, fmt):
    g, p, n, _ = words.shape
    if fmt == "e4m3":
        vals = np.ascontiguousarray(words).view(ml_dtypes.float8_e4m3fn).astype(np.float64)
    else:
        nib = np.empty((g, p, n, 4), np.uint8)
        nib[..., 0::2] = words & 0xF
        nib[..., 1::2] = words >> 4
        vals = E2M1[nib]
    vals = vals * np.repeat(np.exp2(scales.astype(np.float64) - 127.0), 8, axis=1)[..., None]
    return vals.transpose(0, 1, 3, 2).reshape(g * 512, n)
def pack4(w):
    words, scales = pack_weight(w, "e2m1")
    return words.reshape(words.shape[0], 128, -1), scales


def unpack4(words, scales):
    return unpack_weight(words.reshape(words.shape[0], 128, -1, 2), scales, "e2m1")


E4M3FN = np.array([(-1.0 if i & 128 else 1.0) * ((1.0 + (i & 7) / 8.0) * 2.0 ** (((i >> 3) & 15) - 7) if i & 120 else (i & 7) * 2.0 ** -9) for i in range(256)])


def e4m3fn_bytes(y):
    return np.clip(np.asarray(y, np.float64), -448.0, 448.0).astype(np.float32).astype(ml_dtypes.float8_e4m3fn).view(np.uint8)


def e4m3fn_values(b):
    return E4M3FN[b]


B, T, D, F, K, C = 32, 32, 1024, 1024, 8, 128


def draw0():
    s, t = mx_kscale(D), mx_kscale(F)
    z = bf(np.random.standard_normal((B, T, D)) * s)
    w1_words, w1_scales = pack4(np.random.standard_normal((D, F)) / np.sqrt(D) / s[:, None])
    q = bf(np.random.standard_normal((K, F)) * 0.5)
    g = bf((1.0 + 0.1 * np.random.standard_normal(F)) * t)
    w2_words, w2_scales = pack4(np.random.standard_normal((F, C)) / np.sqrt(F) / t[:, None])
    m = bf(np.random.uniform(0.35, 2.8, C) / (K - 1))
    return {
        "z": z,
        "w1_words": w1_words,
        "w1_scales": w1_scales,
        "q": q,
        "g": g,
        "w2_words": w2_words,
        "w2_scales": w2_scales,
        "m": m,
    }


def predict_chunks(z, w1, q, g, w2):
    steps = z.shape[1]
    chunk = q.shape[0]
    u = mxq(z, 2, "e4m3") @ w1
    h = np.concatenate([np.tanh(u[:, :steps - k, :] + q[k]) * g for k in range(chunk)], axis=1)
    y = mxq(h, 2, "e4m3") @ w2
    a = []
    start = 0
    for k in range(chunk):
        a.append(y[:, start:start + steps - k, :])
        start = start + steps - k
    return a


def age_weights(m, steps, chunk):
    t = np.arange(steps)[:, None, None]
    i = np.arange(chunk)[None, :, None]
    w = np.exp(m[None, None, :] * i)
    return np.where(i <= t, w, 0.0)


def delay(x, i):
    return np.concatenate([np.zeros((x.shape[0], i, x.shape[2])), x], axis=1)


def core(z, w1_words, w1_scales, q, g, w2_words, w2_scales, m):
    z, q, g, m = f64(z), f64(q), f64(g), f64(m)
    w1 = unpack4(w1_words, w1_scales)
    w2 = unpack4(w2_words, w2_scales)
    steps = z.shape[1]
    chunk = q.shape[0]
    a = predict_chunks(z, w1, q, g, w2)
    v = age_weights(m, steps, chunk)
    num = np.zeros((z.shape[0], steps, w2.shape[1]))
    for i in range(chunk):
        num = num + v[None, :, i, :] * delay(a[i], i)
    den = np.sum(v, axis=1)
    return num / den[None, :, :]


def setup_inputs():
    drawn = draw0()
    full = np.asarray(drawn['z']).astype(np.float64)
    scale = (np.abs(full).reshape(32, 32, 8, 128).max(axis=(3,)) / 448.0).astype(np.float32)
    given = {}
    for key, value in drawn.items():
        if key == 'z':
            given['z_bytes'] = e4m3fn_bytes(full / np.repeat(scale.astype(np.float64), 128, axis=2))
            given['z_scale'] = scale
        else:
            given[key] = value
    return given


def reference(z_bytes, z_scale, w1_words, w1_scales, q, g, w2_words, w2_scales, m):
    return core(e4m3fn_values(z_bytes) * np.repeat(z_scale.astype(np.float64), 128, axis=2), w1_words, w1_scales, q, g, w2_words, w2_scales, m)

@@ -1,0 +1,389 @@
+from contextlib import ExitStack
+
+import concourse.mybir as mybir
+from concourse.masks import make_identity
+
+B, T, D, F, K, C = 32, 32, 1024, 1024, 8, 128
+FLOPS = 2 * B * T * D * F + 2 * B * (K * T - K * (K - 1) // 2) * F * C
+
+F32 = mybir.dt.float32
+BF16 = mybir.dt.bfloat16
+I32 = mybir.dt.int32
+U32 = mybir.dt.uint32
+U8 = mybir.dt.uint8
+FP8 = mybir.dt.float8_e4m3fn
+FP8X4 = mybir.dt.float8_e4m3fn_x4
+FP4X4 = mybir.dt.float4_e2m1fn_x4
+ACT = mybir.ActivationFunctionType
+ALU = mybir.AluOpType
+
+P = 128
+HB = 16
+HT = HB * T
+UNITS = 16
+RUN = 4
+ACT_BLOCKS = 4
+TH_BUFS = 3
+SPLIT = (5, 6, 7, 8, 13, 14, 15)
+POOL_TOKENS = (424, 312, 248, 224, 288, 312, 288, 272, 328, 264, 248, 224, 288, 312, 288, 272)
+
+
+def tile_acttemporalensembledchunkhead_d1p_kernel(tc, z_bytes, z_scale, w1_words, w1_scales, q, g, w2_words, w2_scales, m, out):
+    nc = tc.nc
+    z_rows = z_bytes.rearrange("b s d -> (b s) d").rearrange("(j p) d -> p j d", p=P)
+    zs_rows = z_scale.rearrange("b s e -> (b s) e").rearrange("(j p) e -> p j e", p=P)
+    out_rows = out.rearrange("b s c -> (b s) c").rearrange("(j p) c -> p j c", p=P)
+    w1_view = w1_words.rearrange("g p n -> p g n")
+
+    with ExitStack() as ctx:
+        sb = ctx.enter_context(tc.tile_pool(name="sb", bufs=1))
+        ps = ctx.enter_context(tc.psum_pool(name="ps", bufs=1))
+        ctx.enter_context(tc.manual_schedule())
+
+        def sbt(name, shape, dtype):
+            return sb.tile(shape, dtype, name=name, align_bytes=64)
+
+        z_raw = [sbt("z_raw%d" % i, [P, 2, D], U8) for i in range(4)]
+        z_sc = [sbt("z_sc%d" % h, [P, 4, 8], F32) for h in range(2)]
+        z_wide = [sbt("z_wide%d" % i, [P, D], BF16) for i in range(8)]
+        z_grp = sbt("z_grp", [P, 2, HT, 4], BF16)
+        z_codes = [sbt("z_codes%d" % h, [P, 2, HT], U32) for h in range(2)]
+        z_mx = [sbt("z_mx%d" % h, [P, 2, HT], U8) for h in range(2)]
+        w1_raw = [sbt("w1_raw%d" % i, [P, 2, 1024], U8) for i in range(2)]
+        w1_cols = [sbt("w1_cols%d" % i, [P, 2, 4, 256], U8) for i in range(2)]
+        w1s_raw = sbt("w1s_raw", [P, 2, F], U8)
+        w1s_cols = [sbt("w1s_cols%d" % i, [P, 2, 4, 128], U8) for i in range(2)]
+        w2_sb = sbt("w2_sb", [P, 2, 256], U8)
+        w2s_sb = sbt("w2s_sb", [P, 2, 128], U8)
+        rows = sbt("rows", [P, 512], BF16)
+        ident = sbt("ident", [P, P], F32)
+        q_sb = sbt("q_sb", [P, 4, 16], F32)
+        g_sb = sbt("g_sb", [P, 2, 4], F32)
+        g_rep = sbt("g_rep", [P, 2, 4, RUN], F32)
+        m_sb = sbt("m_sb", [P, 1], BF16)
+        m_pos = sbt("m_pos", [P, 1], F32)
+        age = sbt("age", [P, K, K], F32)
+        top = sbt("top", [P, K, K], F32)
+        pen = sbt("pen", [P, K, K], F32)
+        arg = sbt("arg", [P, K, K], F32)
+        ex = sbt("ex", [P, K, K], F32)
+        den = sbt("den", [P, K], F32)
+        rden = sbt("rden", [P, K], F32)
+        wts = sbt("wts", [P, K, T], F32)
+        warm = sbt("warm", [P, 2], F32)
+        th = [sbt("th%d" % i, [P, 2, 4, HT], F32) for i in range(TH_BUFS)]
+        h_bf = [sbt("h_bf%d" % i, [P, HT, 4], BF16) for i in range(3)]
+        h_codes = sbt("h_codes", [P, 2, K, HT], U32)
+        h_mx = sbt("h_mx", [P, 2, K, HT], U8)
+        ys = sbt("ys", [P, K, HT], F32)
+        o_sb = [sbt("o_sb%d" % h, [P, 4, C], F32) for h in range(2)]
+
+        u_ps = [ps.tile([P, 512], F32, name="u_ps%d" % i) for i in range(4)]
+        y_ps = [ps.tile([P, 512], F32, name="y_ps%d" % i) for i in range(2)]
+        acc_ps = ps.tile([P, 512], F32, name="acc_ps")
+        g_ps = ps.tile([P, 512], F32, name="g_ps")
+        turn_banks = [y_ps[0], y_ps[1], acc_ps, u_ps[3], y_ps[0], y_ps[1], acc_ps, y_ps[0]]
+
+        nc.vector.memset(rows[:].bitcast(I32), 0)
+        nc.vector.memset(w1s_raw[:].rearrange("p g n -> p (g n)").bitcast(I32), 0)
+        nc.vector.memset(warm[:, 0:1], 0.0)
+        nc.scalar.dma_start(out=z_sc[0][:], in_=zs_rows[:, 0:4, :])
+        nc.scalar.activation(out=warm[:, 1:2], in_=warm[:, 0:1], func=ACT.Exp)
+        nc.sync.dma_start(out=z_raw[0][:], in_=z_rows[:, 0:2, :])
+        nc.sync.dma_start(out=rows[0:16, :], in_=q.rearrange("k (g f) -> (k g) f", g=2))
+        nc.sync.dma_start(out=rows[16:18, :], in_=g.rearrange("(g f) -> g f", g=2))
+        nc.sync.dma_start(out=w1_raw[0][:].bitcast(I32), in_=w1_view[:, :, 0:1024].bitcast(I32))
+        nc.sync.dma_start(out=z_raw[1][:], in_=z_rows[:, 2:4, :])
+        for r in range(4):
+            nc.sync.dma_start(out=w1s_raw[r:P:32, :, :].bitcast(I32), in_=w1_scales[:, r:16:4, :].rearrange("g q n -> q g n").bitcast(I32))
+
+        make_identity(nc, ident[:])
+        nc.gpsimd.iota(age[:], pattern=[[1, K], [0, K]], base=0, channel_multiplier=0, allow_small_or_imprecise_dtypes=True)
+        nc.gpsimd.iota(top[:], pattern=[[0, K], [1, K]], base=0, channel_multiplier=0, allow_small_or_imprecise_dtypes=True)
+        nc.gpsimd.iota(pen[:], pattern=[[-1, K], [1, K]], base=0, channel_multiplier=0, allow_small_or_imprecise_dtypes=True)
+
+        nc.vector.memset(w2s_sb[:].rearrange("p g n -> p (g n)").bitcast(I32), 0)
+        for i in (1, 2):
+            nc.vector.memset(h_bf[i][:, HB * (T - 3):, :].rearrange("p n t -> p (n t)").bitcast(I32), 0)
+        nc.vector.memset(ys[:].rearrange("p k (b s) -> p k b s", s=T)[:, :, :, 0:K], 0.0)
+
+        nc.sync.dma_start(out=z_sc[1][:], in_=zs_rows[:, 4:8, :])
+        nc.sync.dma_start(out=z_raw[2][:], in_=z_rows[:, 4:6, :])
+        nc.sync.dma_start(out=w1_raw[1][:].bitcast(I32), in_=w1_view[:, :, 1024:2048].bitcast(I32))
+        with nc.allow_non_contiguous_dma(reason="one rate a partition"):
+            nc.sync.dma_start(out=m_sb[:], in_=m.rearrange("(c o) -> c o", o=1))
+        nc.sync.dma_start(out=z_raw[3][:], in_=z_rows[:, 6:8, :])
+        nc.sync.dma_start(out=w2_sb[:].bitcast(I32), in_=w2_words.rearrange("g p n -> p g n").bitcast(I32))
+        for r in range(4):
+            nc.sync.dma_start(out=w2s_sb[r:P:32, :, :].bitcast(I32), in_=w2_scales[:, r:16:4, :].rearrange("g q n -> q g n").bitcast(I32))
+
+        def widen(i, act_blocks):
+            src = z_raw[i // 2][:, i % 2, :]
+            for e in range(8):
+                cols = slice(128 * e, 128 * (e + 1))
+                scale = z_sc[i // 4][:, i % 4, e:e + 1]
+                if e < act_blocks:
+                    nc.scalar.activation(out=z_wide[i][:, cols], in_=src[:, cols].bitcast(FP8), func=ACT.Copy, scale=scale)
+                else:
+                    nc.vector.tensor_scalar(out=z_wide[i][:, cols], in0=src[:, cols].bitcast(FP8), scalar1=scale, scalar2=None, op0=ALU.mult)
+
+        def turn(i):
+            words = z_wide[i][:].bitcast(F32)
+            for gp in range(2):
+                for u in range(2):
+                    c0 = 128 * (2 * gp + u)
+                    nc.tensor.transpose(turn_banks[i][:, c0:c0 + 128], words[:, 256 * gp + u:256 * (gp + 1):2], ident[:])
+
+        def turn_out(i, on_scalar):
+            dst = z_grp[:, :, 128 * (i % 4):128 * (i % 4 + 1), :].bitcast(F32)
+            src = turn_banks[i][:].rearrange("p (g u r) -> p g r u", g=2, u=2)
+            if on_scalar:
+                nc.scalar.copy(out=dst, in_=src)
+            else:
+                nc.vector.tensor_copy(out=dst, in_=src)
+
+        def z_quant(h, gp, lo, hi):
+            nc.vector.quantize_mx(
+                out=z_codes[h][:, gp, lo:hi].bitcast(FP8X4),
+                scales=z_mx[h][:, gp, lo:hi],
+                in_=z_grp[:, gp, lo:hi, :].rearrange("p n t -> p (n t)"),
+            )
+
+        def z_quant_tile(i):
+            for gp in range(2):
+                z_quant(0, gp, 128 * i, 128 * (i + 1))
+
+        def w1_order_words(gq):
+            nc.vector.tensor_copy(
+                out=w1_cols[gq][:].rearrange("p g t (m b) -> p g t m b", b=2),
+                in_=w1_raw[gq][:].rearrange("p g (m t b) -> p g t m b", t=4, b=2),
+            )
+
+        def w1_order_scales(gq):
+            nc.vector.tensor_copy(
+                out=w1s_cols[gq][:],
+                in_=w1s_raw[:, :, 512 * gq:512 * (gq + 1)].rearrange("p g (m t) -> p g t m", t=4),
+            )
+
+        def mm1(h, gq, t):
+            for gp in range(2):
+                nc.tensor.matmul_mx(
+                    out=u_ps[t][:],
+                    lhsT=w1_cols[gq][:, gp, t, :].bitcast(FP4X4),
+                    lhsT_scale=w1s_cols[gq][:, gp, t, :],
+                    rhs=z_codes[h][:, gp, :].bitcast(FP8X4),
+                    rhs_scale=z_mx[h][:, gp, :],
+                    start=(gp == 0),
+                    stop=(gp == 1),
+                )
+
+        def unit(n):
+            return n // 8, (n // 4) % 2, 2 * (n % 4)
+
+        def tokens(k):
+            return HB * (T - k)
+
+        def by_batch(ap):
+            return ap.rearrange("p (b s) -> p b s", b=HB)
+
+        def tanh_unit(n):
+            h, gq, ka = unit(n)
+            frees_banks = ka == K - 2 and n + 1 < UNITS
+            if frees_banks:
+                order = [(t, kk) for t in range(4) for kk in range(2)]
+            else:
+                order = [(t, kk) for kk in range(2) for t in range(4)]
+            for t, kk in order:
+                k = ka + kk
+                nc.scalar.activation(
+                    out=by_batch(th[n % TH_BUFS][:, kk, t, 0:tokens(k)]),
+                    in_=by_batch(u_ps[t][:])[:, :, 0:T - k],
+                    func=ACT.Tanh,
+                    bias=q_sb[:, t, 2 * k + gq:2 * k + gq + 1],
+                )
+                if frees_banks and kk == 1:
+                    mm1(unit(n + 1)[0], unit(n + 1)[1], t)
+
+        def h_tile(n, kk):
+            return h_bf[kk * (1 + n % 2)]
+
+        def gain_vector(n, kk, lo, hi):
+            g0 = 256 + 4 * RUN * unit(n)[1]
+            nc.vector.tensor_tensor(
+                out=h_tile(n, kk)[:, lo:hi, :].rearrange("p (c i) t -> p c t i", i=RUN),
+                in0=th[n % TH_BUFS][:, kk, :, lo:hi].rearrange("p t (c i) -> p c t i", i=RUN),
+                in1=g_ps[:, g0:g0 + 4 * RUN].rearrange("p (t i) -> p t i", i=RUN).unsqueeze(1).to_broadcast([P, (hi - lo) // RUN, 4, RUN]),
+                op=ALU.mult,
+            )
+
+        def gain_pool(n, hi):
+            nc.gpsimd.tensor_tensor(
+                out=h_tile(n, 0)[:, 0:hi, :],
+                in0=th[n % TH_BUFS][:, 0, :, 0:hi].rearrange("p t n -> p n t"),
+                in1=g_sb[:, unit(n)[1], :].unsqueeze(1).to_broadcast([P, hi, 4]),
+                op=ALU.mult,
+            )
+
+        def h_quant(n, kk):
+            h, gq, ka = unit(n)
+            nc.vector.quantize_mx(
+                out=h_codes[:, gq, ka + kk, :].bitcast(FP8X4),
+                scales=h_mx[:, gq, ka + kk, :],
+                in_=h_tile(n, kk)[:].rearrange("p n t -> p (n t)"),
+            )
+
+        def mm2(k, gq):
+            nc.tensor.matmul_mx(
+                out=y_ps[k % 2][:],
+                lhsT=w2_sb[:, gq, :].bitcast(FP4X4),
+                lhsT_scale=w2s_sb[:, gq, :],
+                rhs=h_codes[:, gq, k, :].bitcast(FP8X4),
+                rhs_scale=h_mx[:, gq, k, :],
+                start=(gq == 0),
+                stop=(gq == 1),
+            )
+
+        def weigh_vector(k, end):
+            nc.vector.tensor_tensor(
+                out=by_batch(ys[:, k, :])[:, :, k:end],
+                in0=by_batch(y_ps[k % 2][:, 0:tokens(k)])[:, :, 0:end - k],
+                in1=wts[:, k, k:end].unsqueeze(1).to_broadcast([P, HB, end - k]),
+                op=ALU.mult,
+            )
+
+        def weigh_scalar(k):
+            nc.scalar.activation(
+                out=by_batch(ys[:, k, :])[:, :, K - 1:T],
+                in_=by_batch(y_ps[k % 2][:, 0:tokens(k)])[:, :, K - 1 - k:T - k],
+                func=ACT.Copy,
+                scale=wts[:, k, K - 1:K],
+            )
+
+        def gather(k):
+            for i in range(4):
+                nc.tensor.matmul(
+                    acc_ps[:, 128 * i:128 * (i + 1)],
+                    lhsT=ys[:, k, 128 * i:128 * (i + 1)],
+                    rhs=ident[:],
+                    start=(k == 0 and i == 0),
+                    stop=(k == K - 1 and i == 3),
+                    is_transpose=True,
+                )
+
+        def finish(h):
+            nc.scalar.copy(out=o_sb[h][:].rearrange("p i c -> p (i c)"), in_=acc_ps[:])
+            nc.sync.dma_start(out=out_rows[:, 4 * h:4 * h + 4, :], in_=o_sb[h][:])
+
+        def flat(ap):
+            return ap.rearrange("p k s -> p (k s)")
+
+        def pe_warm(count):
+            for i in range(count):
+                nc.tensor.matmul(u_ps[2][:, 0:P], lhsT=ident[:], rhs=ident[:], start=True, stop=True)
+
+        pe_warm(3)
+        row_words = rows[:].bitcast(F32)
+        for u in range(2):
+            nc.tensor.transpose(g_ps[:, 128 * u:128 * (u + 1)], row_words[:, u:256:2], ident[:])
+        turned = g_ps[:, 0:256].bitcast(BF16).rearrange("p (u r e) -> p u e r", u=2, e=2)
+        for i in range(4):
+            widen(i, ACT_BLOCKS)
+            pe_warm(1)
+            turn(i)
+            if i == 1:
+                nc.vector.tensor_copy(out=q_sb[:].rearrange("p (u e) r -> p u e r", u=2), in_=turned[:, :, :, 0:16])
+                nc.vector.tensor_copy(out=g_sb[:].rearrange("p g (u e) -> p u e g", u=2), in_=turned[:, :, :, 16:18])
+            if i == 2:
+                nc.vector.tensor_copy(out=g_rep[:], in_=g_sb[:].unsqueeze(3).to_broadcast([P, 2, 4, RUN]))
+        nc.tensor.matmul(g_ps[:, 256:256 + 8 * RUN], lhsT=ident[:], rhs=g_rep[:].rearrange("p g t i -> p (g t i)"), start=True, stop=True)
+        turn_out(0, True)
+        w1_order_words(0)
+        turn_out(1, True)
+        z_quant_tile(0)
+        turn_out(2, True)
+        w1_order_scales(0)
+        z_quant_tile(1)
+        turn_out(3, True)
+        z_quant_tile(2)
+        z_quant_tile(3)
+        pe_warm(1)
+        for t in range(4):
+            mm1(0, 0, t)
+
+        widen(4, 8)
+        turn(4)
+        tanh_unit(0)
+        nc.vector.tensor_scalar(out=pen[:], in0=pen[:], scalar1=0.0, scalar2=30000.0, op0=ALU.min, op1=ALU.mult)
+        nc.vector.tensor_scalar(out=m_pos[:], in0=m_sb[:], scalar1=0.0, scalar2=None, op0=ALU.max)
+        widen(5, 0)
+        turn(5)
+        nc.vector.scalar_tensor_tensor(out=flat(top[:]), in0=flat(top[:]), scalar=m_pos[:], in1=flat(pen[:]), op0=ALU.mult, op1=ALU.subtract)
+        widen(6, 0)
+        turn(6)
+        nc.vector.scalar_tensor_tensor(out=flat(arg[:]), in0=flat(age[:]), scalar=m_sb[:], in1=flat(top[:]), op0=ALU.mult, op1=ALU.subtract)
+        widen(7, 0)
+        w1_order_words(1)
+        nc.scalar.activation(out=ex[:], in_=arg[:], func=ACT.Exp)
+
+        for n in range(UNITS + 1):
+            weighs = n >= 1 and unit(n - 1)[1] == 1
+            ky = unit(n - 1)[2]
+            ka = unit(n)[2]
+            opens = n < UNITS and unit(n)[1] == 1
+            if weighs:
+                mm2(ky, 1)
+                mm2(ky + 1, 1)
+            if n + 1 < UNITS:
+                tanh_unit(n + 1)
+            if n >= 2 and unit(n - 2)[1] == 1:
+                gather(unit(n - 2)[2])
+                gather(unit(n - 2)[2] + 1)
+            if n == 10:
+                finish(0)
+            if n == UNITS:
+                weigh_vector(ky, T)
+                gather(ky)
+                weigh_vector(ky + 1, T)
+                gather(ky + 1)
+                finish(1)
+                continue
+            share = POOL_TOKENS[n]
+            gain_pool(n, share)
+            if weighs:
+                gain_vector(n, 1, 0, tokens(ka + 1))
+                if n in SPLIT:
+                    weigh_vector(ky, K - 1)
+                    weigh_scalar(ky)
+                else:
+                    weigh_vector(ky, T)
+                if opens:
+                    mm2(ka, 0)
+                gain_vector(n, 0, share, tokens(ka))
+                weigh_vector(ky + 1, T)
+                if opens:
+                    mm2(ka + 1, 0)
+            else:
+                if opens:
+                    mm2(ka, 0)
+                    mm2(ka + 1, 0)
+                gain_vector(n, 0, share, tokens(ka))
+                if n == 0:
+                    turn_out(4, False)
+                    turn(7)
+                    turn_out(5, False)
+                gain_vector(n, 1, 0, tokens(ka + 1))
+            if n < 2:
+                turn_out(6 + n, False)
+            if n == 1:
+                nc.vector.tensor_reduce(out=den[:], in_=ex[:].rearrange("p k s -> p s k"), axis=mybir.AxisListType.X, op=ALU.add)
+                w1_order_scales(1)
+            if n == 2:
+                nc.vector.reciprocal(out=rden[:], in_=den[:])
+            if n == 3:
+                nc.vector.tensor_tensor(out=wts[:, :, 0:K], in0=ex[:], in1=rden[:].unsqueeze(1).to_broadcast([P, K, K]), op=ALU.mult)
+            if n == 4:
+                nc.vector.tensor_copy(out=wts[:, :, K:T], in_=wts[:, :, K - 1:K].to_broadcast([P, K, T - K]))
+            if n in (2, 3):
+                z_quant(1, n - 2, 0, HT)
+            h_quant(n, 0)
+            h_quant(n, 1)

@@ -25,7 +25,7 @@ RUN = 4
 ACT_BLOCKS = 4
 TH_BUFS = 3
 SPLIT = (5, 6, 7, 8, 13, 14, 15)
-POOL_TOKENS = (424, 312, 248, 224, 288, 312, 288, 272, 328, 264, 248, 224, 288, 312, 288, 272)
+POOL_TOKENS = (392, 288, 232, 208, 264, 288, 272, 248, 304, 248, 232, 208, 264, 288, 272, 248)
 
 
 def tile_acttemporalensembledchunkhead_d1p_kernel(tc, z_bytes, z_scale, w1_words, w1_scales, q, g, w2_words, w2_scales, m, out):
@@ -70,7 +70,6 @@ def tile_acttemporalensembledchunkhead_d1p_kernel(tc, z_bytes, z_scale, w1_words
         den = sbt("den", [P, K], F32)
         rden = sbt("rden", [P, K], F32)
         wts = sbt("wts", [P, K, T], F32)
-        warm = sbt("warm", [P, 2], F32)
         th = [sbt("th%d" % i, [P, 2, 4, HT], F32) for i in range(TH_BUFS)]
         h_bf = [sbt("h_bf%d" % i, [P, HT, 4], BF16) for i in range(3)]
         h_codes = sbt("h_codes", [P, 2, K, HT], U32)
@@ -86,9 +85,10 @@ def tile_acttemporalensembledchunkhead_d1p_kernel(tc, z_bytes, z_scale, w1_words
 
         nc.vector.memset(rows[:].bitcast(I32), 0)
         nc.vector.memset(w1s_raw[:].rearrange("p g n -> p (g n)").bitcast(I32), 0)
-        nc.vector.memset(warm[:, 0:1], 0.0)
         nc.scalar.dma_start(out=z_sc[0][:], in_=zs_rows[:, 0:4, :])
-        nc.scalar.activation(out=warm[:, 1:2], in_=warm[:, 0:1], func=ACT.Exp)
+        nc.gpsimd.iota(pen[:], pattern=[[1, K], [-1, K]], base=0, channel_multiplier=0, allow_small_or_imprecise_dtypes=True)
+        nc.vector.tensor_scalar(out=pen[:], in0=pen[:], scalar1=0.0, scalar2=0.75, op0=ALU.is_gt, op1=ALU.subtract)
+        nc.scalar.activation(out=pen[:], in_=pen[:], func=ACT.Exp, scale=80.0)
         nc.sync.dma_start(out=z_raw[0][:], in_=z_rows[:, 0:2, :])
         nc.sync.dma_start(out=rows[0:16, :], in_=q.rearrange("k (g f) -> (k g) f", g=2))
         nc.sync.dma_start(out=rows[16:18, :], in_=g.rearrange("(g f) -> g f", g=2))
@@ -100,7 +100,6 @@ def tile_acttemporalensembledchunkhead_d1p_kernel(tc, z_bytes, z_scale, w1_words
         make_identity(nc, ident[:])
         nc.gpsimd.iota(age[:], pattern=[[1, K], [0, K]], base=0, channel_multiplier=0, allow_small_or_imprecise_dtypes=True)
         nc.gpsimd.iota(top[:], pattern=[[0, K], [1, K]], base=0, channel_multiplier=0, allow_small_or_imprecise_dtypes=True)
-        nc.gpsimd.iota(pen[:], pattern=[[-1, K], [1, K]], base=0, channel_multiplier=0, allow_small_or_imprecise_dtypes=True)
 
         nc.vector.memset(w2s_sb[:].rearrange("p g n -> p (g n)").bitcast(I32), 0)
         for i in (1, 2):
@@ -243,11 +242,11 @@ def tile_acttemporalensembledchunkhead_d1p_kernel(tc, z_bytes, z_scale, w1_words
                 stop=(gq == 1),
             )
 
-        def weigh_vector(k, end):
+        def weigh_vector(k, end, b0=0, b1=HB):
             nc.vector.tensor_tensor(
-                out=by_batch(ys[:, k, :])[:, :, k:end],
-                in0=by_batch(y_ps[k % 2][:, 0:tokens(k)])[:, :, 0:end - k],
-                in1=wts[:, k, k:end].unsqueeze(1).to_broadcast([P, HB, end - k]),
+                out=by_batch(ys[:, k, :])[:, b0:b1, k:end],
+                in0=by_batch(y_ps[k % 2][:, 0:tokens(k)])[:, b0:b1, 0:end - k],
+                in1=wts[:, k, k:end].unsqueeze(1).to_broadcast([P, b1 - b0, end - k]),
                 op=ALU.mult,
             )
 
@@ -259,14 +258,18 @@ def tile_acttemporalensembledchunkhead_d1p_kernel(tc, z_bytes, z_scale, w1_words
                 scale=wts[:, k, K - 1:K],
             )
 
-        def gather(k):
-            for i in range(4):
+        def acc_bank(h, i):
+            return (acc_ps, 0, 3) if h == 0 else (u_ps[i // 2], i // 2 * 2, i // 2 * 2 + 1)
+
+        def gather(h, k, tiles):
+            for i in tiles:
+                bank, first, last = acc_bank(h, i)
                 nc.tensor.matmul(
-                    acc_ps[:, 128 * i:128 * (i + 1)],
+                    bank[:, 128 * (i - first):128 * (i - first + 1)],
                     lhsT=ys[:, k, 128 * i:128 * (i + 1)],
                     rhs=ident[:],
-                    start=(k == 0 and i == 0),
-                    stop=(k == K - 1 and i == 3),
+                    start=(k == 0 and i == first),
+                    stop=(k == K - 1 and i == last),
                     is_transpose=True,
                 )
 
@@ -313,11 +316,10 @@ def tile_acttemporalensembledchunkhead_d1p_kernel(tc, z_bytes, z_scale, w1_words
         widen(4, 8)
         turn(4)
         tanh_unit(0)
-        nc.vector.tensor_scalar(out=pen[:], in0=pen[:], scalar1=0.0, scalar2=30000.0, op0=ALU.min, op1=ALU.mult)
         nc.vector.tensor_scalar(out=m_pos[:], in0=m_sb[:], scalar1=0.0, scalar2=None, op0=ALU.max)
         widen(5, 0)
         turn(5)
-        nc.vector.scalar_tensor_tensor(out=flat(top[:]), in0=flat(top[:]), scalar=m_pos[:], in1=flat(pen[:]), op0=ALU.mult, op1=ALU.subtract)
+        nc.vector.scalar_tensor_tensor(out=flat(top[:]), in0=flat(top[:]), scalar=m_pos[:], in1=flat(pen[:]), op0=ALU.mult, op1=ALU.add)
         widen(6, 0)
         turn(6)
         nc.vector.scalar_tensor_tensor(out=flat(arg[:]), in0=flat(age[:]), scalar=m_sb[:], in1=flat(top[:]), op0=ALU.mult, op1=ALU.subtract)
@@ -336,16 +338,20 @@ def tile_acttemporalensembledchunkhead_d1p_kernel(tc, z_bytes, z_scale, w1_words
             if n + 1 < UNITS:
                 tanh_unit(n + 1)
             if n >= 2 and unit(n - 2)[1] == 1:
-                gather(unit(n - 2)[2])
-                gather(unit(n - 2)[2] + 1)
+                gather(unit(n - 2)[0], unit(n - 2)[2], range(4))
+                gather(unit(n - 2)[0], unit(n - 2)[2] + 1, range(4))
             if n == 10:
                 finish(0)
             if n == UNITS:
                 weigh_vector(ky, T)
-                gather(ky)
-                weigh_vector(ky + 1, T)
-                gather(ky + 1)
-                finish(1)
+                gather(1, ky, range(4))
+                for a in range(2):
+                    weigh_vector(ky + 1, T, 8 * a, 8 * a + 8)
+                    gather(1, ky + 1, (2 * a, 2 * a + 1))
+                nc.scalar.copy(out=o_sb[1][:, 0:2, :].rearrange("p i c -> p (i c)"), in_=u_ps[0][:, 0:256])
+                nc.scalar.dma_start(out=out_rows[:, 4:6, :], in_=o_sb[1][:, 0:2, :])
+                nc.vector.tensor_copy(out=o_sb[1][:, 2:4, :].rearrange("p i c -> p (i c)"), in_=u_ps[1][:, 0:256])
+                nc.sync.dma_start(out=out_rows[:, 6:8, :], in_=o_sb[1][:, 2:4, :])
                 continue
             share = POOL_TOKENS[n]
             gain_pool(n, share)

@@ -25,7 +25,8 @@ RUN = 4
 ACT_BLOCKS = 4
 TH_BUFS = 3
 SPLIT = (5, 6, 7, 8, 13, 14, 15)
-POOL_TOKENS = (392, 288, 232, 208, 264, 288, 272, 248, 304, 248, 232, 208, 264, 288, 272, 248)
+SPLIT_BOTH = (14, 15)
+POOL_TOKENS = (440, 320, 256, 232, 296, 320, 296, 280, 344, 272, 256, 232, 296, 320, 272, 248)
 
 
 def tile_acttemporalensembledchunkhead_d1p_kernel(tc, z_bytes, z_scale, w1_words, w1_scales, q, g, w2_words, w2_scales, m, out):
@@ -280,18 +281,12 @@ def tile_acttemporalensembledchunkhead_d1p_kernel(tc, z_bytes, z_scale, w1_words
         def flat(ap):
             return ap.rearrange("p k s -> p (k s)")
 
-        def pe_warm(count):
-            for i in range(count):
-                nc.tensor.matmul(u_ps[2][:, 0:P], lhsT=ident[:], rhs=ident[:], start=True, stop=True)
-
-        pe_warm(3)
         row_words = rows[:].bitcast(F32)
         for u in range(2):
             nc.tensor.transpose(g_ps[:, 128 * u:128 * (u + 1)], row_words[:, u:256:2], ident[:])
         turned = g_ps[:, 0:256].bitcast(BF16).rearrange("p (u r e) -> p u e r", u=2, e=2)
         for i in range(4):
             widen(i, ACT_BLOCKS)
-            pe_warm(1)
             turn(i)
             if i == 1:
                 nc.vector.tensor_copy(out=q_sb[:].rearrange("p (u e) r -> p u e r", u=2), in_=turned[:, :, :, 0:16])
@@ -309,7 +304,6 @@ def tile_acttemporalensembledchunkhead_d1p_kernel(tc, z_bytes, z_scale, w1_words
         turn_out(3, True)
         z_quant_tile(2)
         z_quant_tile(3)
-        pe_warm(1)
         for t in range(4):
             mm1(0, 0, t)
 
@@ -338,7 +332,8 @@ def tile_acttemporalensembledchunkhead_d1p_kernel(tc, z_bytes, z_scale, w1_words
             if n + 1 < UNITS:
                 tanh_unit(n + 1)
             if n >= 2 and unit(n - 2)[1] == 1:
-                gather(unit(n - 2)[0], unit(n - 2)[2], range(4))
+                if n < UNITS:
+                    gather(unit(n - 2)[0], unit(n - 2)[2], range(4))
                 gather(unit(n - 2)[0], unit(n - 2)[2] + 1, range(4))
             if n == 10:
                 finish(0)
@@ -364,8 +359,14 @@ def tile_acttemporalensembledchunkhead_d1p_kernel(tc, z_bytes, z_scale, w1_words
                     weigh_vector(ky, T)
                 if opens:
                     mm2(ka, 0)
+                if n == UNITS - 1:
+                    gather(1, ky, range(4))
                 gain_vector(n, 0, share, tokens(ka))
-                weigh_vector(ky + 1, T)
+                if n in SPLIT_BOTH:
+                    weigh_vector(ky + 1, K - 1)
+                    weigh_scalar(ky + 1)
+                else:
+                    weigh_vector(ky + 1, T)
                 if opens:
                     mm2(ka + 1, 0)
             else:

@@ -117,22 +117,32 @@ def tile_acttemporalensembledchunkhead_d1p_kernel(tc, z_bytes, z_scale, w1_words
         for r in range(4):
             nc.sync.dma_start(out=w2s_sb[r:P:32, :, :].bitcast(I32), in_=w2_scales[:, r:16:4, :].rearrange("g q n -> q g n").bitcast(I32))
 
-        def widen(i, act_blocks):
+        def widen(i, act_blocks, sort):
             src = z_raw[i // 2][:, i % 2, :]
             for e in range(8):
                 cols = slice(128 * e, 128 * (e + 1))
                 scale = z_sc[i // 4][:, i % 4, e:e + 1]
                 if e < act_blocks:
                     nc.scalar.activation(out=z_wide[i][:, cols], in_=src[:, cols].bitcast(FP8), func=ACT.Copy, scale=scale)
-                else:
+                elif not sort:
                     nc.vector.tensor_scalar(out=z_wide[i][:, cols], in0=src[:, cols].bitcast(FP8), scalar1=scale, scalar2=None, op0=ALU.mult)
+                else:
+                    sorted_words = z_wide[i][:, 512 * (e // 4):512 * (e // 4 + 1)].rearrange("p (u w e) -> p w u e", u=2, e=2)
+                    nc.vector.tensor_scalar(
+                        out=sorted_words[:, 32 * (e % 4):32 * (e % 4 + 1), :, :],
+                        in0=src[:, cols].bitcast(FP8).rearrange("p (w u e) -> p w u e", u=2, e=2),
+                        scalar1=scale,
+                        scalar2=None,
+                        op0=ALU.mult,
+                    )
 
-        def turn(i):
+        def turn(i, act_blocks):
             words = z_wide[i][:].bitcast(F32)
             for gp in range(2):
                 for u in range(2):
                     c0 = 128 * (2 * gp + u)
-                    nc.tensor.transpose(turn_banks[i][:, c0:c0 + 128], words[:, 256 * gp + u:256 * (gp + 1):2], ident[:])
+                    src = words[:, 256 * gp + u:256 * (gp + 1):2] if 4 * gp < act_blocks else words[:, c0:c0 + 128]
+                    nc.tensor.transpose(turn_banks[i][:, c0:c0 + 128], src, ident[:])
 
         def turn_out(i, on_scalar):
             dst = z_grp[:, :, 128 * (i % 4):128 * (i % 4 + 1), :].bitcast(F32)
@@ -152,6 +162,8 @@ def tile_acttemporalensembledchunkhead_d1p_kernel(tc, z_bytes, z_scale, w1_words
         def z_quant_tile(i):
             for gp in range(2):
                 z_quant(0, gp, 128 * i, 128 * (i + 1))
+            for t in range(2):
+                mm1(0, 0, t, 128 * i, 128 * (i + 1))
 
         def w1_order_words(gq):
             nc.vector.tensor_copy(
@@ -165,14 +177,14 @@ def tile_acttemporalensembledchunkhead_d1p_kernel(tc, z_bytes, z_scale, w1_words
                 in_=w1s_raw[:, :, 512 * gq:512 * (gq + 1)].rearrange("p g (m t) -> p g t m", t=4),
             )
 
-        def mm1(h, gq, t):
+        def mm1(h, gq, t, lo=0, hi=HT):
             for gp in range(2):
                 nc.tensor.matmul_mx(
-                    out=u_ps[t][:],
+                    out=u_ps[t][:, lo:hi],
                     lhsT=w1_cols[gq][:, gp, t, :].bitcast(FP4X4),
                     lhsT_scale=w1s_cols[gq][:, gp, t, :],
-                    rhs=z_codes[h][:, gp, :].bitcast(FP8X4),
-                    rhs_scale=z_mx[h][:, gp, :],
+                    rhs=z_codes[h][:, gp, lo:hi].bitcast(FP8X4),
+                    rhs_scale=z_mx[h][:, gp, lo:hi],
                     start=(gp == 0),
                     stop=(gp == 1),
                 )
@@ -286,38 +298,38 @@ def tile_acttemporalensembledchunkhead_d1p_kernel(tc, z_bytes, z_scale, w1_words
             nc.tensor.transpose(g_ps[:, 128 * u:128 * (u + 1)], row_words[:, u:256:2], ident[:])
         turned = g_ps[:, 0:256].bitcast(BF16).rearrange("p (u r e) -> p u e r", u=2, e=2)
         for i in range(4):
-            widen(i, ACT_BLOCKS)
-            turn(i)
+            widen(i, ACT_BLOCKS, True)
+            turn(i, ACT_BLOCKS)
             if i == 1:
                 nc.vector.tensor_copy(out=q_sb[:].rearrange("p (u e) r -> p u e r", u=2), in_=turned[:, :, :, 0:16])
                 nc.vector.tensor_copy(out=g_sb[:].rearrange("p g (u e) -> p u e g", u=2), in_=turned[:, :, :, 16:18])
             if i == 2:
                 nc.vector.tensor_copy(out=g_rep[:], in_=g_sb[:].unsqueeze(3).to_broadcast([P, 2, 4, RUN]))
-        nc.tensor.matmul(g_ps[:, 256:256 + 8 * RUN], lhsT=ident[:], rhs=g_rep[:].rearrange("p g t i -> p (g t i)"), start=True, stop=True)
         turn_out(0, True)
         w1_order_words(0)
         turn_out(1, True)
+        w1_order_scales(0)
         z_quant_tile(0)
         turn_out(2, True)
-        w1_order_scales(0)
         z_quant_tile(1)
         turn_out(3, True)
         z_quant_tile(2)
         z_quant_tile(3)
-        for t in range(4):
+        for t in range(2, 4):
             mm1(0, 0, t)
+        nc.tensor.matmul(g_ps[:, 256:256 + 8 * RUN], lhsT=ident[:], rhs=g_rep[:].rearrange("p g t i -> p (g t i)"), start=True, stop=True)
 
-        widen(4, 8)
-        turn(4)
+        widen(4, 8, False)
+        turn(4, 8)
         tanh_unit(0)
         nc.vector.tensor_scalar(out=m_pos[:], in0=m_sb[:], scalar1=0.0, scalar2=None, op0=ALU.max)
-        widen(5, 0)
-        turn(5)
+        widen(5, 0, False)
+        turn(5, 8)
         nc.vector.scalar_tensor_tensor(out=flat(top[:]), in0=flat(top[:]), scalar=m_pos[:], in1=flat(pen[:]), op0=ALU.mult, op1=ALU.add)
-        widen(6, 0)
-        turn(6)
+        widen(6, 0, False)
+        turn(6, 8)
         nc.vector.scalar_tensor_tensor(out=flat(arg[:]), in0=flat(age[:]), scalar=m_sb[:], in1=flat(top[:]), op0=ALU.mult, op1=ALU.subtract)
-        widen(7, 0)
+        widen(7, 0, False)
         w1_order_words(1)
         nc.scalar.activation(out=ex[:], in_=arg[:], func=ACT.Exp)
 
@@ -328,6 +340,8 @@ def tile_acttemporalensembledchunkhead_d1p_kernel(tc, z_bytes, z_scale, w1_words
             opens = n < UNITS and unit(n)[1] == 1
             if weighs:
                 mm2(ky, 1)
+                if n == UNITS:
+                    mm2(ky + 1, 0)
                 mm2(ky + 1, 1)
             if n + 1 < UNITS:
                 tanh_unit(n + 1)
@@ -367,7 +381,7 @@ def tile_acttemporalensembledchunkhead_d1p_kernel(tc, z_bytes, z_scale, w1_words
                     weigh_scalar(ky + 1)
                 else:
                     weigh_vector(ky + 1, T)
-                if opens:
+                if opens and n < UNITS - 1:
                     mm2(ka + 1, 0)
             else:
                 if opens:
@@ -376,7 +390,7 @@ def tile_acttemporalensembledchunkhead_d1p_kernel(tc, z_bytes, z_scale, w1_words
                 gain_vector(n, 0, share, tokens(ka))
                 if n == 0:
                     turn_out(4, False)
-                    turn(7)
+                    turn(7, 8)
                     turn_out(5, False)
                 gain_vector(n, 1, 0, tokens(ka + 1))
             if n < 2:

from contextlib import ExitStack

import concourse.mybir as mybir
from concourse.masks import make_identity

B, T, D, F, K, C = 32, 32, 1024, 1024, 8, 128
FLOPS = 2 * B * T * D * F + 2 * B * (K * T - K * (K - 1) // 2) * F * C

F32 = mybir.dt.float32
BF16 = mybir.dt.bfloat16
I32 = mybir.dt.int32
U32 = mybir.dt.uint32
U8 = mybir.dt.uint8
FP8 = mybir.dt.float8_e4m3fn
FP8X4 = mybir.dt.float8_e4m3fn_x4
FP4X4 = mybir.dt.float4_e2m1fn_x4
ACT = mybir.ActivationFunctionType
ALU = mybir.AluOpType

P = 128
HB = 16
HT = HB * T
UNITS = 16
RUN = 4
ACT_BLOCKS = 4
TH_BUFS = 3
SPLIT = (5, 6, 7, 8, 13, 14, 15)
SPLIT_BOTH = (14, 15)
POOL_TOKENS = (440, 320, 256, 232, 296, 320, 296, 280, 344, 272, 256, 232, 296, 320, 272, 248)


def tile_acttemporalensembledchunkhead_d1p_kernel(tc, z_bytes, z_scale, w1_words, w1_scales, q, g, w2_words, w2_scales, m, out):
    nc = tc.nc
    z_rows = z_bytes.rearrange("b s d -> (b s) d").rearrange("(j p) d -> p j d", p=P)
    zs_rows = z_scale.rearrange("b s e -> (b s) e").rearrange("(j p) e -> p j e", p=P)
    out_rows = out.rearrange("b s c -> (b s) c").rearrange("(j p) c -> p j c", p=P)
    w1_view = w1_words.rearrange("g p n -> p g n")

    with ExitStack() as ctx:
        sb = ctx.enter_context(tc.tile_pool(name="sb", bufs=1))
        ps = ctx.enter_context(tc.psum_pool(name="ps", bufs=1))
        ctx.enter_context(tc.manual_schedule())

        def sbt(name, shape, dtype):
            return sb.tile(shape, dtype, name=name, align_bytes=64)

        z_raw = [sbt("z_raw%d" % i, [P, 2, D], U8) for i in range(4)]
        z_sc = [sbt("z_sc%d" % h, [P, 4, 8], F32) for h in range(2)]
        z_wide = [sbt("z_wide%d" % i, [P, D], BF16) for i in range(8)]
        z_grp = sbt("z_grp", [P, 2, HT, 4], BF16)
        z_codes = [sbt("z_codes%d" % h, [P, 2, HT], U32) for h in range(2)]
        z_mx = [sbt("z_mx%d" % h, [P, 2, HT], U8) for h in range(2)]
        w1_raw = [sbt("w1_raw%d" % i, [P, 2, 1024], U8) for i in range(2)]
        w1_cols = [sbt("w1_cols%d" % i, [P, 2, 4, 256], U8) for i in range(2)]
        w1s_raw = sbt("w1s_raw", [P, 2, F], U8)
        w1s_cols = [sbt("w1s_cols%d" % i, [P, 2, 4, 128], U8) for i in range(2)]
        w2_sb = sbt("w2_sb", [P, 2, 256], U8)
        w2s_sb = sbt("w2s_sb", [P, 2, 128], U8)
        rows = sbt("rows", [P, 512], BF16)
        ident = sbt("ident", [P, P], F32)
        q_sb = sbt("q_sb", [P, 4, 16], F32)
        g_sb = sbt("g_sb", [P, 2, 4], F32)
        g_rep = sbt("g_rep", [P, 2, 4, RUN], F32)
        m_sb = sbt("m_sb", [P, 1], BF16)
        m_pos = sbt("m_pos", [P, 1], F32)
        age = sbt("age", [P, K, K], F32)
        top = sbt("top", [P, K, K], F32)
        pen = sbt("pen", [P, K, K], F32)
        arg = sbt("arg", [P, K, K], F32)
        ex = sbt("ex", [P, K, K], F32)
        den = sbt("den", [P, K], F32)
        rden = sbt("rden", [P, K], F32)
        wts = sbt("wts", [P, K, T], F32)
        th = [sbt("th%d" % i, [P, 2, 4, HT], F32) for i in range(TH_BUFS)]
        h_bf = [sbt("h_bf%d" % i, [P, HT, 4], BF16) for i in range(3)]
        h_codes = sbt("h_codes", [P, 2, K, HT], U32)
        h_mx = sbt("h_mx", [P, 2, K, HT], U8)
        ys = sbt("ys", [P, K, HT], F32)
        o_sb = [sbt("o_sb%d" % h, [P, 4, C], F32) for h in range(2)]

        u_ps = [ps.tile([P, 512], F32, name="u_ps%d" % i) for i in range(4)]
        y_ps = [ps.tile([P, 512], F32, name="y_ps%d" % i) for i in range(2)]
        acc_ps = ps.tile([P, 512], F32, name="acc_ps")
        g_ps = ps.tile([P, 512], F32, name="g_ps")
        turn_banks = [y_ps[0], y_ps[1], acc_ps, u_ps[3], y_ps[0], y_ps[1], acc_ps, y_ps[0]]

        nc.vector.memset(rows[:].bitcast(I32), 0)
        nc.vector.memset(w1s_raw[:].rearrange("p g n -> p (g n)").bitcast(I32), 0)
        nc.scalar.dma_start(out=z_sc[0][:], in_=zs_rows[:, 0:4, :])
        nc.gpsimd.iota(pen[:], pattern=[[1, K], [-1, K]], base=0, channel_multiplier=0, allow_small_or_imprecise_dtypes=True)
        nc.vector.tensor_scalar(out=pen[:], in0=pen[:], scalar1=0.0, scalar2=0.75, op0=ALU.is_gt, op1=ALU.subtract)
        nc.scalar.activation(out=pen[:], in_=pen[:], func=ACT.Exp, scale=80.0)
        nc.sync.dma_start(out=z_raw[0][:], in_=z_rows[:, 0:2, :])
        nc.sync.dma_start(out=rows[0:16, :], in_=q.rearrange("k (g f) -> (k g) f", g=2))
        nc.sync.dma_start(out=rows[16:18, :], in_=g.rearrange("(g f) -> g f", g=2))
        nc.sync.dma_start(out=w1_raw[0][:].bitcast(I32), in_=w1_view[:, :, 0:1024].bitcast(I32))
        nc.sync.dma_start(out=z_raw[1][:], in_=z_rows[:, 2:4, :])
        for r in range(4):
            nc.sync.dma_start(out=w1s_raw[r:P:32, :, :].bitcast(I32), in_=w1_scales[:, r:16:4, :].rearrange("g q n -> q g n").bitcast(I32))

        make_identity(nc, ident[:])
        nc.gpsimd.iota(age[:], pattern=[[1, K], [0, K]], base=0, channel_multiplier=0, allow_small_or_imprecise_dtypes=True)
        nc.gpsimd.iota(top[:], pattern=[[0, K], [1, K]], base=0, channel_multiplier=0, allow_small_or_imprecise_dtypes=True)

        nc.vector.memset(w2s_sb[:].rearrange("p g n -> p (g n)").bitcast(I32), 0)
        for i in (1, 2):
            nc.vector.memset(h_bf[i][:, HB * (T - 3):, :].rearrange("p n t -> p (n t)").bitcast(I32), 0)
        nc.vector.memset(ys[:].rearrange("p k (b s) -> p k b s", s=T)[:, :, :, 0:K], 0.0)

        nc.sync.dma_start(out=z_sc[1][:], in_=zs_rows[:, 4:8, :])
        nc.sync.dma_start(out=z_raw[2][:], in_=z_rows[:, 4:6, :])
        nc.sync.dma_start(out=w1_raw[1][:].bitcast(I32), in_=w1_view[:, :, 1024:2048].bitcast(I32))
        with nc.allow_non_contiguous_dma(reason="one rate a partition"):
            nc.sync.dma_start(out=m_sb[:], in_=m.rearrange("(c o) -> c o", o=1))
        nc.sync.dma_start(out=z_raw[3][:], in_=z_rows[:, 6:8, :])
        nc.sync.dma_start(out=w2_sb[:].bitcast(I32), in_=w2_words.rearrange("g p n -> p g n").bitcast(I32))
        for r in range(4):
            nc.sync.dma_start(out=w2s_sb[r:P:32, :, :].bitcast(I32), in_=w2_scales[:, r:16:4, :].rearrange("g q n -> q g n").bitcast(I32))

        def widen(i, act_blocks, sort):
            src = z_raw[i // 2][:, i % 2, :]
            for e in range(8):
                cols = slice(128 * e, 128 * (e + 1))
                scale = z_sc[i // 4][:, i % 4, e:e + 1]
                if e < act_blocks:
                    nc.scalar.activation(out=z_wide[i][:, cols], in_=src[:, cols].bitcast(FP8), func=ACT.Copy, scale=scale)
                elif not sort:
                    nc.vector.tensor_scalar(out=z_wide[i][:, cols], in0=src[:, cols].bitcast(FP8), scalar1=scale, scalar2=None, op0=ALU.mult)
                else:
                    sorted_words = z_wide[i][:, 512 * (e // 4):512 * (e // 4 + 1)].rearrange("p (u w e) -> p w u e", u=2, e=2)
                    nc.vector.tensor_scalar(
                        out=sorted_words[:, 32 * (e % 4):32 * (e % 4 + 1), :, :],
                        in0=src[:, cols].bitcast(FP8).rearrange("p (w u e) -> p w u e", u=2, e=2),
                        scalar1=scale,
                        scalar2=None,
                        op0=ALU.mult,
                    )

        def turn(i, act_blocks):
            words = z_wide[i][:].bitcast(F32)
            for gp in range(2):
                for u in range(2):
                    c0 = 128 * (2 * gp + u)
                    src = words[:, 256 * gp + u:256 * (gp + 1):2] if 4 * gp < act_blocks else words[:, c0:c0 + 128]
                    nc.tensor.transpose(turn_banks[i][:, c0:c0 + 128], src, ident[:])

        def turn_out(i, on_scalar):
            dst = z_grp[:, :, 128 * (i % 4):128 * (i % 4 + 1), :].bitcast(F32)
            src = turn_banks[i][:].rearrange("p (g u r) -> p g r u", g=2, u=2)
            if on_scalar:
                nc.scalar.copy(out=dst, in_=src)
            else:
                nc.vector.tensor_copy(out=dst, in_=src)

        def z_quant(h, gp, lo, hi):
            nc.vector.quantize_mx(
                out=z_codes[h][:, gp, lo:hi].bitcast(FP8X4),
                scales=z_mx[h][:, gp, lo:hi],
                in_=z_grp[:, gp, lo:hi, :].rearrange("p n t -> p (n t)"),
            )

        def z_quant_tile(i):
            for gp in range(2):
                z_quant(0, gp, 128 * i, 128 * (i + 1))
            for t in range(2):
                mm1(0, 0, t, 128 * i, 128 * (i + 1))

        def w1_order_words(gq):
            nc.vector.tensor_copy(
                out=w1_cols[gq][:].rearrange("p g t (m b) -> p g t m b", b=2),
                in_=w1_raw[gq][:].rearrange("p g (m t b) -> p g t m b", t=4, b=2),
            )

        def w1_order_scales(gq):
            nc.vector.tensor_copy(
                out=w1s_cols[gq][:],
                in_=w1s_raw[:, :, 512 * gq:512 * (gq + 1)].rearrange("p g (m t) -> p g t m", t=4),
            )

        def mm1(h, gq, t, lo=0, hi=HT):
            for gp in range(2):
                nc.tensor.matmul_mx(
                    out=u_ps[t][:, lo:hi],
                    lhsT=w1_cols[gq][:, gp, t, :].bitcast(FP4X4),
                    lhsT_scale=w1s_cols[gq][:, gp, t, :],
                    rhs=z_codes[h][:, gp, lo:hi].bitcast(FP8X4),
                    rhs_scale=z_mx[h][:, gp, lo:hi],
                    start=(gp == 0),
                    stop=(gp == 1),
                )

        def unit(n):
            return n // 8, (n // 4) % 2, 2 * (n % 4)

        def tokens(k):
            return HB * (T - k)

        def by_batch(ap):
            return ap.rearrange("p (b s) -> p b s", b=HB)

        def tanh_unit(n):
            h, gq, ka = unit(n)
            frees_banks = ka == K - 2 and n + 1 < UNITS
            if frees_banks:
                order = [(t, kk) for t in range(4) for kk in range(2)]
            else:
                order = [(t, kk) for kk in range(2) for t in range(4)]
            for t, kk in order:
                k = ka + kk
                nc.scalar.activation(
                    out=by_batch(th[n % TH_BUFS][:, kk, t, 0:tokens(k)]),
                    in_=by_batch(u_ps[t][:])[:, :, 0:T - k],
                    func=ACT.Tanh,
                    bias=q_sb[:, t, 2 * k + gq:2 * k + gq + 1],
                )
                if frees_banks and kk == 1:
                    mm1(unit(n + 1)[0], unit(n + 1)[1], t)

        def h_tile(n, kk):
            return h_bf[kk * (1 + n % 2)]

        def gain_vector(n, kk, lo, hi):
            g0 = 256 + 4 * RUN * unit(n)[1]
            nc.vector.tensor_tensor(
                out=h_tile(n, kk)[:, lo:hi, :].rearrange("p (c i) t -> p c t i", i=RUN),
                in0=th[n % TH_BUFS][:, kk, :, lo:hi].rearrange("p t (c i) -> p c t i", i=RUN),
                in1=g_ps[:, g0:g0 + 4 * RUN].rearrange("p (t i) -> p t i", i=RUN).unsqueeze(1).to_broadcast([P, (hi - lo) // RUN, 4, RUN]),
                op=ALU.mult,
            )

        def gain_pool(n, hi):
            nc.gpsimd.tensor_tensor(
                out=h_tile(n, 0)[:, 0:hi, :],
                in0=th[n % TH_BUFS][:, 0, :, 0:hi].rearrange("p t n -> p n t"),
                in1=g_sb[:, unit(n)[1], :].unsqueeze(1).to_broadcast([P, hi, 4]),
                op=ALU.mult,
            )

        def h_quant(n, kk):
            h, gq, ka = unit(n)
            nc.vector.quantize_mx(
                out=h_codes[:, gq, ka + kk, :].bitcast(FP8X4),
                scales=h_mx[:, gq, ka + kk, :],
                in_=h_tile(n, kk)[:].rearrange("p n t -> p (n t)"),
            )

        def mm2(k, gq):
            nc.tensor.matmul_mx(
                out=y_ps[k % 2][:],
                lhsT=w2_sb[:, gq, :].bitcast(FP4X4),
                lhsT_scale=w2s_sb[:, gq, :],
                rhs=h_codes[:, gq, k, :].bitcast(FP8X4),
                rhs_scale=h_mx[:, gq, k, :],
                start=(gq == 0),
                stop=(gq == 1),
            )

        def weigh_vector(k, end, b0=0, b1=HB):
            nc.vector.tensor_tensor(
                out=by_batch(ys[:, k, :])[:, b0:b1, k:end],
                in0=by_batch(y_ps[k % 2][:, 0:tokens(k)])[:, b0:b1, 0:end - k],
                in1=wts[:, k, k:end].unsqueeze(1).to_broadcast([P, b1 - b0, end - k]),
                op=ALU.mult,
            )

        def weigh_scalar(k):
            nc.scalar.activation(
                out=by_batch(ys[:, k, :])[:, :, K - 1:T],
                in_=by_batch(y_ps[k % 2][:, 0:tokens(k)])[:, :, K - 1 - k:T - k],
                func=ACT.Copy,
                scale=wts[:, k, K - 1:K],
            )

        def acc_bank(h, i):
            return (acc_ps, 0, 3) if h == 0 else (u_ps[i // 2], i // 2 * 2, i // 2 * 2 + 1)

        def gather(h, k, tiles):
            for i in tiles:
                bank, first, last = acc_bank(h, i)
                nc.tensor.matmul(
                    bank[:, 128 * (i - first):128 * (i - first + 1)],
                    lhsT=ys[:, k, 128 * i:128 * (i + 1)],
                    rhs=ident[:],
                    start=(k == 0 and i == first),
                    stop=(k == K - 1 and i == last),
                    is_transpose=True,
                )

        def finish(h):
            nc.scalar.copy(out=o_sb[h][:].rearrange("p i c -> p (i c)"), in_=acc_ps[:])
            nc.sync.dma_start(out=out_rows[:, 4 * h:4 * h + 4, :], in_=o_sb[h][:])

        def flat(ap):
            return ap.rearrange("p k s -> p (k s)")

        row_words = rows[:].bitcast(F32)
        for u in range(2):
            nc.tensor.transpose(g_ps[:, 128 * u:128 * (u + 1)], row_words[:, u:256:2], ident[:])
        turned = g_ps[:, 0:256].bitcast(BF16).rearrange("p (u r e) -> p u e r", u=2, e=2)
        for i in range(4):
            widen(i, ACT_BLOCKS, True)
            turn(i, ACT_BLOCKS)
            if i == 1:
                nc.vector.tensor_copy(out=q_sb[:].rearrange("p (u e) r -> p u e r", u=2), in_=turned[:, :, :, 0:16])
                nc.vector.tensor_copy(out=g_sb[:].rearrange("p g (u e) -> p u e g", u=2), in_=turned[:, :, :, 16:18])
            if i == 2:
                nc.vector.tensor_copy(out=g_rep[:], in_=g_sb[:].unsqueeze(3).to_broadcast([P, 2, 4, RUN]))
        turn_out(0, True)
        w1_order_words(0)
        turn_out(1, True)
        w1_order_scales(0)
        z_quant_tile(0)
        turn_out(2, True)
        z_quant_tile(1)
        turn_out(3, True)
        z_quant_tile(2)
        z_quant_tile(3)
        for t in range(2, 4):
            mm1(0, 0, t)
        nc.tensor.matmul(g_ps[:, 256:256 + 8 * RUN], lhsT=ident[:], rhs=g_rep[:].rearrange("p g t i -> p (g t i)"), start=True, stop=True)

        widen(4, 8, False)
        turn(4, 8)
        tanh_unit(0)
        nc.vector.tensor_scalar(out=m_pos[:], in0=m_sb[:], scalar1=0.0, scalar2=None, op0=ALU.max)
        widen(5, 0, False)
        turn(5, 8)
        nc.vector.scalar_tensor_tensor(out=flat(top[:]), in0=flat(top[:]), scalar=m_pos[:], in1=flat(pen[:]), op0=ALU.mult, op1=ALU.add)
        widen(6, 0, False)
        turn(6, 8)
        nc.vector.scalar_tensor_tensor(out=flat(arg[:]), in0=flat(age[:]), scalar=m_sb[:], in1=flat(top[:]), op0=ALU.mult, op1=ALU.subtract)
        widen(7, 0, False)
        w1_order_words(1)
        nc.scalar.activation(out=ex[:], in_=arg[:], func=ACT.Exp)

        for n in range(UNITS + 1):
            weighs = n >= 1 and unit(n - 1)[1] == 1
            ky = unit(n - 1)[2]
            ka = unit(n)[2]
            opens = n < UNITS and unit(n)[1] == 1
            if weighs:
                mm2(ky, 1)
                if n == UNITS:
                    mm2(ky + 1, 0)
                mm2(ky + 1, 1)
            if n + 1 < UNITS:
                tanh_unit(n + 1)
            if n >= 2 and unit(n - 2)[1] == 1:
                if n < UNITS:
                    gather(unit(n - 2)[0], unit(n - 2)[2], range(4))
                gather(unit(n - 2)[0], unit(n - 2)[2] + 1, range(4))
            if n == 10:
                finish(0)
            if n == UNITS:
                weigh_vector(ky, T)
                gather(1, ky, range(4))
                for a in range(2):
                    weigh_vector(ky + 1, T, 8 * a, 8 * a + 8)
                    gather(1, ky + 1, (2 * a, 2 * a + 1))
                nc.scalar.copy(out=o_sb[1][:, 0:2, :].rearrange("p i c -> p (i c)"), in_=u_ps[0][:, 0:256])
                nc.scalar.dma_start(out=out_rows[:, 4:6, :], in_=o_sb[1][:, 0:2, :])
                nc.vector.tensor_copy(out=o_sb[1][:, 2:4, :].rearrange("p i c -> p (i c)"), in_=u_ps[1][:, 0:256])
                nc.sync.dma_start(out=out_rows[:, 6:8, :], in_=o_sb[1][:, 2:4, :])
                continue
            share = POOL_TOKENS[n]
            gain_pool(n, share)
            if weighs:
                gain_vector(n, 1, 0, tokens(ka + 1))
                if n in SPLIT:
                    weigh_vector(ky, K - 1)
                    weigh_scalar(ky)
                else:
                    weigh_vector(ky, T)
                if opens:
                    mm2(ka, 0)
                if n == UNITS - 1:
                    gather(1, ky, range(4))
                gain_vector(n, 0, share, tokens(ka))
                if n in SPLIT_BOTH:
                    weigh_vector(ky + 1, K - 1)
                    weigh_scalar(ky + 1)
                else:
                    weigh_vector(ky + 1, T)
                if opens and n < UNITS - 1:
                    mm2(ka + 1, 0)
            else:
                if opens:
                    mm2(ka, 0)
                    mm2(ka + 1, 0)
                gain_vector(n, 0, share, tokens(ka))
                if n == 0:
                    turn_out(4, False)
                    turn(7, 8)
                    turn_out(5, False)
                gain_vector(n, 1, 0, tokens(ka + 1))
            if n < 2:
                turn_out(6 + n, False)
            if n == 1:
                nc.vector.tensor_reduce(out=den[:], in_=ex[:].rearrange("p k s -> p s k"), axis=mybir.AxisListType.X, op=ALU.add)
                w1_order_scales(1)
            if n == 2:
                nc.vector.reciprocal(out=rden[:], in_=den[:])
            if n == 3:
                nc.vector.tensor_tensor(out=wts[:, :, 0:K], in0=ex[:], in1=rden[:].unsqueeze(1).to_broadcast([P, K, K]), op=ALU.mult)
            if n == 4:
                nc.vector.tensor_copy(out=wts[:, :, K:T], in_=wts[:, :, K - 1:K].to_broadcast([P, K, T - K]))
            if n in (2, 3):
                z_quant(1, n - 2, 0, HT)
            h_quant(n, 0)
            h_quant(n, 1)
